import numpy as np
import ml_dtypes


def mxq(x, axis, fmt="e4m3"):
    dtype, down = {"e4m3": (ml_dtypes.float8_e4m3fn, 7), "e5m2": (ml_dtypes.float8_e5m2, 14)}[fmt]
    v = np.moveaxis(np.asarray(x, np.float32).astype(ml_dtypes.bfloat16).astype(np.float64), axis, -1)
    blocks = v.reshape(v.shape[:-1] + (-1, 32))
    amax = np.abs(blocks).max(-1, keepdims=True)
    byte = np.maximum(np.where(amax > 0, np.frexp(amax)[1] - 1 + 127, 0) - down, 1)
    scale = np.exp2(byte - 127.0)
    codes = (blocks / scale).astype(np.float32).astype(dtype).astype(np.float64)
    return np.moveaxis((codes * scale).reshape(v.shape), -1, axis)


WIDE = False


def mx_kscale(k):
    if not WIDE:
        return np.ones(k)
    levels = np.array([10, -10, 5, -5, 0])
    if k % 512:
        return np.exp2(np.random.permutation(np.resize(levels, k // 32))).repeat(32)
    a = np.empty((k // 512, 16))
    for p in range(k // 512):
        a[p, :8] = np.random.permutation(np.resize(levels, 8))
        for g in range(8):
            far = levels[np.abs(levels - a[p, g]) >= 10]
            a[p, g + 8] = far[np.random.randint(len(far))]
    return np.exp2(a.ravel()).repeat(32)


def f64(x):
    return np.asarray(x).astype(np.float64)


def striped8(idx):
    return np.asarray(idx).reshape(8, -1, 16).transpose(0, 2, 1).reshape(128, -1).astype(np.uint16)


def unstriped8(offs):
    return offs.reshape(8, 16, -1).transpose(0, 2, 1).reshape(8, -1).astype(np.int64)


def pick8(x, idx, run):
    r = np.arange(len(x))
    return x[r[:, None], idx[r % (8 * run) // run]]


E2M1 = np.array([0.0, 0.5, 1.0, 1.5, 2.0, 3.0, 4.0, 6.0, -0.0, -0.5, -1.0, -1.5, -2.0, -3.0, -4.0, -6.0])


def pack_weight(w, fmt):
    k, n = w.shape
    w = f64(np.asarray(w, np.float32).astype(ml_dtypes.bfloat16)).reshape(k // 32, 32, n)
    amax = np.abs(w).max(1)
    if fmt == "e4m3":
        byte = np.frexp(amax)[1] - 1 + 127 - 7
    else:
        mant, ex = np.frexp(amax / 6.0)
        byte = np.where(mant > 0.5, ex, ex - 1) + 127
    byte = np.clip(np.where(amax > 0, byte, 1), 1, 254)
    scaled = (w * np.exp2(127.0 - byte)[:, None, :]).reshape(k, n).astype(np.float32)
    by_word = np.ascontiguousarray(scaled.reshape(k // 512, 128, 4, n).transpose(0, 1, 3, 2))
    if fmt == "e4m3":
        words = by_word.astype(ml_dtypes.float8_e4m3fn).view(np.uint8)
    else:
        c = by_word.astype(ml_dtypes.float4_e2m1fn).view(np.uint8) & 0xF
        words = (c[..., 0::2] | (c[..., 1::2] << 4)).reshape(k // 512, 128, 2 * n)
    return np.ascontiguousarray(words), np.ascontiguousarray(byte.astype(np.uint8).reshape(k // 512, 16, n))


def unpack_weight(words, scales, fmt):
    g, _, n = scales.shape
    words = np.ascontiguousarray(words).reshape(g, 128, n, -1)
    if fmt == "e4m3":
        vals = words.view(ml_dtypes.float8_e4m3fn).astype(np.float64)
    else:
        nib = np.empty((g, 128, n, 4), np.uint8)
        nib[..., 0::2] = words & 0xF
        nib[..., 1::2] = words >> 4
        vals = E2M1[nib]
    vals = vals * np.repeat(np.exp2(scales.astype(np.float64) - 127.0), 8, axis=1)[..., None]
    return vals.transpose(0, 1, 3, 2).reshape(g * 512, n)


def bf(x):
    return np.asarray(x, np.float32).astype(ml_dtypes.bfloat16)


def planes(Y):
    r, m = Y.shape
    b = f64(bf(Y)).reshape(r // 32, 32, m)
    amax = np.abs(b).max(1)
    byte = np.clip(np.where(amax > 0, np.frexp(amax)[1] - 1 + 127 - 7, 1), 1, 254)
    codes = (b * np.exp2(127.0 - byte)[:, None, :]).reshape(r, m).astype(np.float32).astype(ml_dtypes.float8_e4m3fn).view(np.uint8)
    words = codes.reshape(r // 512, 128, 4, m).transpose(0, 1, 3, 2)
    return np.ascontiguousarray(words), np.ascontiguousarray(byte.astype(np.uint8).reshape(r // 512, 16, m))


K, T, J, B, L, N = 512, 512, 512, 128, 512, 512


def setup_inputs():
    n = np.random.standard_normal
    idx = np.stack([np.random.randint(0, T, J) for _ in range(8)])
    fk = mx_kscale(K)
    fl = mx_kscale(L)
    xtp = pack_weight(n((K, T)) / fk[:, None], "e2m1")
    sxp = pack_weight(n((L, J)) / fl[:, None], "e4m3")
    wsp = pack_weight(n((L, N)) * 1 / np.sqrt(L) * fl[:, None], "e2m1")
    return {
        "xt_words": xtp[0],
        "xt_scales": xtp[1],
        "w": (n((K, N)) * 1 / np.sqrt(K) * fk[:, None]).astype(np.float32),
        "sx_words": sxp[0],
        "sx_scales": sxp[1],
        "ws_words": wsp[0],
        "ws_scales": wsp[1],
        "offs": striped8(idx),
    }


def reference(xt_words, xt_scales, w, sx_words, sx_scales, ws_words, ws_scales, offs):
    idx = unstriped8(offs)
    xtu = unpack_weight(xt_words, xt_scales, "e2m1")
    sxu = unpack_weight(sx_words, sx_scales, "e4m3")
    wsu = unpack_weight(ws_words, ws_scales, "e2m1")
    wq = mxq(f64(w), 0, "e4m3")
    z = wq.T @ xtu
    u = pick8(z, idx, 64)
    m = u.reshape(N, B, J // B).mean(axis=2)
    mr = np.repeat(m, J // B, axis=1)
    q = wsu.T @ sxu
    y = np.tanh(u - mr) + 0.5 * q
    words, scales = planes(y)
    return y, words, scales

@@ -1,0 +1,191 @@
+from contextlib import ExitStack
+
+import concourse.mybir as mybir
+
+F32 = mybir.dt.float32
+BF16 = mybir.dt.bfloat16
+I32 = mybir.dt.int32
+U32 = mybir.dt.uint32
+U16 = mybir.dt.uint16
+U8 = mybir.dt.uint8
+FP8X4 = mybir.dt.float8_e4m3fn_x4
+FP4X4 = mybir.dt.float4_e2m1fn_x4
+ADD = mybir.AluOpType.add
+MULT = mybir.AluOpType.mult
+TANH = mybir.ActivationFunctionType.Tanh
+
+P = 128
+PACK = 4
+K = T = J = L = N = 512
+GROUP = 4
+FLOPS = 2 * K * N * T + 2 * L * N * J
+CHUNKS = ((0, 256), (256, 128), (384, 128))
+
+
+def load_scales(queue, plane, rows):
+    for quad in range(4):
+        queue.dma_start(out=plane[32 * quad : 32 * quad + 4, :].bitcast(I32), in_=rows[0, 4 * quad : 4 * quad + 4, :].bitcast(I32))
+
+
+def tile_list_head_members_and_group_pl_kernel(tc, xt_words, xt_scales, w, sx_words, sx_scales, ws_words, ws_scales, offs, out_0, out_1, out_2):
+    nc = tc.nc
+    with ExitStack() as ctx:
+        keep = ctx.enter_context(tc.tile_pool(name="keep", bufs=1))
+        psum = ctx.enter_context(tc.psum_pool(name="psum", bufs=1))
+
+        lists = keep.tile([P, J // 16], U16, name="lists")
+        ws_plane = keep.tile([P, N], U8, name="ws_plane", align_bytes=64)
+        xt_plane = keep.tile([P, T], U8, name="xt_plane", align_bytes=64)
+        sx_plane = keep.tile([P, J], U8, name="sx_plane", align_bytes=64)
+        for plane in (ws_plane, xt_plane, sx_plane):
+            nc.vector.memset(plane[:].bitcast(I32), 0)
+
+        ws_raw = keep.tile([P, 2 * N], U8, name="ws_raw", align_bytes=64)
+        xt_codes = keep.tile([P, 2 * T], U8, name="xt_codes", align_bytes=64)
+        sx_codes = keep.tile([P, J], U32, name="sx_codes", align_bytes=64)
+        w_rows = w.rearrange("(p r) n -> p r n", r=PACK)
+        w_raw = [keep.tile([P, PACK, N // 2], F32, name="w_raw%d" % h) for h in range(2)]
+
+        nc.sync.dma_start(out=ws_raw[:].bitcast(I32), in_=ws_words[0].bitcast(I32))
+        load_scales(nc.sync, ws_plane, ws_scales)
+        for h in range(2):
+            nc.sync.dma_start(out=w_raw[h][:], in_=w_rows[:, :, h * (N // 2) : (h + 1) * (N // 2)])
+        nc.sync.dma_start(out=xt_codes[:].bitcast(I32), in_=xt_words[0].bitcast(I32))
+        load_scales(nc.sync, xt_plane, xt_scales)
+        nc.sync.dma_start(lists[:], offs)
+        nc.sync.dma_start(out=sx_codes[:].bitcast(I32), in_=sx_words[0].rearrange("p c r -> p (c r)").bitcast(I32))
+        load_scales(nc.sync, sx_plane, sx_scales)
+
+        ws_codes = keep.tile([P, 2 * N], U8, name="ws_codes", align_bytes=64)
+        ws_dealt_plane = keep.tile([P, N], U8, name="ws_dealt_plane", align_bytes=64)
+        nc.vector.tensor_copy(out=ws_codes[:].rearrange("p (t m b) -> p t m b", t=PACK, b=2), in_=ws_raw[:].rearrange("p (m t b) -> p t m b", t=PACK, b=2))
+        nc.vector.tensor_copy(out=ws_dealt_plane[:].rearrange("p (t m) -> p t m", t=PACK), in_=ws_plane[:].rearrange("p (m t) -> p t m", t=PACK))
+
+        w_bf = keep.tile([P, PACK, P, PACK], BF16, name="w_bf", align_bytes=64)
+        for h in range(2):
+            nc.vector.tensor_copy(
+                out=w_bf[:, :, h * 64 : (h + 1) * 64, :].rearrange("p t m r -> p m r t"),
+                in_=w_raw[h][:].rearrange("p r (m t) -> p m r t", t=PACK),
+            )
+        z = []
+        for t in range(PACK):
+            w_codes = keep.tile([P, P], U32, name="w_codes%d" % t, align_bytes=64)
+            w_plane = keep.tile([P, P], U8, name="w_plane%d" % t, align_bytes=64)
+            nc.vector.quantize_mx(out=w_codes[:].bitcast(FP8X4), scales=w_plane[:], in_=w_bf[:, t, :, :].rearrange("p m r -> p (m r)"))
+            z_bank = psum.tile([P, T], F32, name="z_bank%d" % t)
+            nc.tensor.matmul_mx(out=z_bank[:], lhsT=w_codes[:].bitcast(FP8X4), lhsT_scale=w_plane[:], rhs=xt_codes[:].bitcast(FP4X4), rhs_scale=xt_plane[:], start=True, stop=True)
+            z_t = keep.tile([P, T], F32, name="z%d" % t)
+            nc.scalar.copy(out=z_t[:], in_=z_bank[:])
+            z.append(z_t)
+
+        q_banks = []
+        for c, (j0, width) in enumerate(CHUNKS):
+            per_bank = 512 // width
+            banks = []
+            for b in range(PACK // per_bank):
+                bank = psum.tile([P, per_bank, width], F32, name="q_bank%d_%d" % (c, b))
+                for i in range(per_bank):
+                    t = b * per_bank + i
+                    nc.tensor.matmul_mx(
+                        out=bank[:, i, :],
+                        lhsT=ws_codes[:, 2 * P * t : 2 * P * (t + 1)].bitcast(FP4X4),
+                        lhsT_scale=ws_dealt_plane[:, P * t : P * (t + 1)],
+                        rhs=sx_codes[:, j0 : j0 + width].bitcast(FP8X4),
+                        rhs_scale=sx_plane[:, j0 : j0 + width],
+                        start=True,
+                        stop=True,
+                    )
+                banks.append(bank)
+            q_banks.append(banks)
+
+        y_plane = keep.tile([P, J], U8, name="y_plane", align_bytes=64)
+        out_rows = out_0.rearrange("(p t) j -> p t j", t=PACK)
+        out_words = out_1[0].rearrange("p c r -> p (c r)").bitcast(I32)
+        tiles = []
+        for c, (j0, width) in enumerate(CHUNKS):
+            d = {}
+            for key in ("u", "d", "th", "y"):
+                d[key] = keep.tile([P, PACK, width], F32, name="%s%d" % (key, c))
+            d["pair"] = keep.tile([P, width, 2], F32, name="pair%d" % c)
+            d["sum"] = keep.tile([P, width], F32, name="sum%d" % c)
+            d["bf"] = keep.tile([P, width, PACK], BF16, name="bf%d" % c, align_bytes=64)
+            d["codes"] = keep.tile([P, width], U32, name="codes%d" % c, align_bytes=64)
+            tiles.append(d)
+
+        def gather(c, t):
+            j0, width = CHUNKS[c]
+            nc.vector.tensor_copy(tiles[c]["u"][:, t, :], z[t][:].indirect(lists[:, j0 // 16 : (j0 + width) // 16]))
+
+        def members(ap):
+            return ap.rearrange("p t (b g) -> p (t b) g", g=GROUP)
+
+        def pairs(c):
+            u = members(tiles[c]["u"][:])
+            nc.vector.tensor_tensor(tiles[c]["pair"][:], u[:, :, 0:2], u[:, :, 2:4], ADD)
+
+        def sums(c):
+            pr = tiles[c]["pair"]
+            nc.vector.tensor_tensor(tiles[c]["sum"][:], pr[:, :, 0], pr[:, :, 1], ADD)
+
+        def centre(c):
+            width = CHUNKS[c][1]
+            nc.vector.scalar_tensor_tensor(
+                out=members(tiles[c]["d"][:]),
+                in0=tiles[c]["sum"][:].unsqueeze(2).to_broadcast([P, width, GROUP]),
+                scalar=-1.0 / GROUP,
+                in1=members(tiles[c]["u"][:]),
+                op0=MULT,
+                op1=ADD,
+            )
+            nc.scalar.activation(out=tiles[c]["th"][:], in_=tiles[c]["d"][:], func=TANH)
+
+        def add_q(c, b):
+            per_bank = 512 // CHUNKS[c][1]
+            ts = slice(b * per_bank, (b + 1) * per_bank)
+            nc.vector.scalar_tensor_tensor(out=tiles[c]["y"][:, ts, :], in0=q_banks[c][b][:], scalar=0.5, in1=tiles[c]["th"][:, ts, :], op0=MULT, op1=ADD)
+
+        def store_y(c, engine_copy):
+            j0, width = CHUNKS[c]
+            nc.sync.dma_start(out=out_rows[:, :, j0 : j0 + width], in_=tiles[c]["y"][:])
+            engine_copy(
+                out=tiles[c]["bf"][:].rearrange("p (c i) t -> p c t i", i=4),
+                in_=tiles[c]["y"][:].rearrange("p t (c i) -> p c t i", i=4),
+            )
+
+        def planes(c):
+            j0, width = CHUNKS[c]
+            nc.vector.quantize_mx(out=tiles[c]["codes"][:].bitcast(FP8X4), scales=y_plane[:, j0 : j0 + width], in_=tiles[c]["bf"][:].rearrange("p c t -> p (c t)"))
+            nc.sync.dma_start(out=out_words[:, j0 : j0 + width], in_=tiles[c]["codes"][:].bitcast(I32))
+
+        for t in range(PACK):
+            gather(0, t)
+        gather(1, 0)
+        pairs(0)
+        gather(1, 1)
+        sums(0)
+        gather(1, 2)
+        centre(0)
+        gather(1, 3)
+        gather(2, 0)
+        pairs(1)
+        gather(2, 1)
+        sums(1)
+        gather(2, 2)
+        centre(1)
+        gather(2, 3)
+        add_q(0, 0)
+        pairs(2)
+        add_q(0, 1)
+        store_y(0, nc.scalar.copy)
+        sums(2)
+        add_q(1, 0)
+        store_y(1, nc.scalar.copy)
+        centre(2)
+        planes(0)
+        add_q(2, 0)
+        planes(1)
+        store_y(2, nc.vector.tensor_copy)
+        planes(2)
+        for quad in range(4):
+            queue = nc.scalar if quad % 2 else nc.sync
+            queue.dma_start(out=out_2[0, 4 * quad : 4 * quad + 4, :].bitcast(I32), in_=y_plane[32 * quad : 32 * quad + 4, :].bitcast(I32))

@@ -1,6 +1,7 @@
 from contextlib import ExitStack
 
 import concourse.mybir as mybir
+from concourse.masks import make_identity
 
 F32 = mybir.dt.float32
 BF16 = mybir.dt.bfloat16
@@ -13,13 +14,17 @@ FP4X4 = mybir.dt.float4_e2m1fn_x4
 ADD = mybir.AluOpType.add
 MULT = mybir.AluOpType.mult
 TANH = mybir.ActivationFunctionType.Tanh
+COPY = mybir.ActivationFunctionType.Copy
 
 P = 128
 PACK = 4
 K = T = J = L = N = 512
 GROUP = 4
 FLOPS = 2 * K * N * T + 2 * L * N * J
-CHUNKS = ((0, 256), (256, 128), (384, 128))
+HALF = J // 2
+W_SPLIT = 88
+Y_SPLIT = 176
+Z_REST = 64
 
 
 def load_scales(queue, plane, rows):
@@ -34,158 +39,158 @@ def tile_list_head_members_and_group_pl_kernel(tc, xt_words, xt_scales, w, sx_wo
         psum = ctx.enter_context(tc.psum_pool(name="psum", bufs=1))
 
         lists = keep.tile([P, J // 16], U16, name="lists")
-        ws_plane = keep.tile([P, N], U8, name="ws_plane", align_bytes=64)
+        ws_plane = keep.tile([P, N], U8, name="ws_plane", tag="stage_b", align_bytes=64)
         xt_plane = keep.tile([P, T], U8, name="xt_plane", align_bytes=64)
-        sx_plane = keep.tile([P, J], U8, name="sx_plane", align_bytes=64)
-        for plane in (ws_plane, xt_plane, sx_plane):
-            nc.vector.memset(plane[:].bitcast(I32), 0)
+        nc.gpsimd.memset(ws_plane[:].bitcast(I32), 0)
+        identity = keep.tile([P, P], F32, name="identity")
+        make_identity(nc, identity[:])
 
-        ws_raw = keep.tile([P, 2 * N], U8, name="ws_raw", align_bytes=64)
+        ws_raw = keep.tile([P, 2 * N], U8, name="ws_raw", tag="stage_s", align_bytes=64)
         xt_codes = keep.tile([P, 2 * T], U8, name="xt_codes", align_bytes=64)
-        sx_codes = keep.tile([P, J], U32, name="sx_codes", align_bytes=64)
         w_rows = w.rearrange("(p r) n -> p r n", r=PACK)
-        w_raw = [keep.tile([P, PACK, N // 2], F32, name="w_raw%d" % h) for h in range(2)]
+        w_raw = keep.tile([P, PACK, N], F32, name="w_raw", tag="stage_w", align_bytes=64)
 
-        nc.sync.dma_start(out=ws_raw[:].bitcast(I32), in_=ws_words[0].bitcast(I32))
-        load_scales(nc.sync, ws_plane, ws_scales)
-        for h in range(2):
-            nc.sync.dma_start(out=w_raw[h][:], in_=w_rows[:, :, h * (N // 2) : (h + 1) * (N // 2)])
-        nc.sync.dma_start(out=xt_codes[:].bitcast(I32), in_=xt_words[0].bitcast(I32))
-        load_scales(nc.sync, xt_plane, xt_scales)
+        sx_codes = keep.tile([P, J], U32, name="sx_codes", align_bytes=64)
         nc.sync.dma_start(lists[:], offs)
+        load_scales(nc.scalar, xt_plane, xt_scales)
+        nc.sync.dma_start(out=ws_raw[:].bitcast(I32), in_=ws_words[0].bitcast(I32))
+        nc.sync.dma_start(out=xt_codes[:].bitcast(I32), in_=xt_words[0].bitcast(I32))
+        nc.sync.dma_start(out=w_raw[:], in_=w_rows)
         nc.sync.dma_start(out=sx_codes[:].bitcast(I32), in_=sx_words[0].rearrange("p c r -> p (c r)").bitcast(I32))
-        load_scales(nc.sync, sx_plane, sx_scales)
+        load_scales(nc.scalar, ws_plane, ws_scales)
 
         ws_codes = keep.tile([P, 2 * N], U8, name="ws_codes", align_bytes=64)
         ws_dealt_plane = keep.tile([P, N], U8, name="ws_dealt_plane", align_bytes=64)
         nc.vector.tensor_copy(out=ws_codes[:].rearrange("p (t m b) -> p t m b", t=PACK, b=2), in_=ws_raw[:].rearrange("p (m t b) -> p t m b", t=PACK, b=2))
-        nc.vector.tensor_copy(out=ws_dealt_plane[:].rearrange("p (t m) -> p t m", t=PACK), in_=ws_plane[:].rearrange("p (m t) -> p t m", t=PACK))
+        sx_plane = keep.tile([P, J], U8, name="sx_plane", tag="stage_s", align_bytes=64)
+        load_scales(nc.sync, sx_plane, sx_scales)
 
         w_bf = keep.tile([P, PACK, P, PACK], BF16, name="w_bf", align_bytes=64)
-        for h in range(2):
-            nc.vector.tensor_copy(
-                out=w_bf[:, :, h * 64 : (h + 1) * 64, :].rearrange("p t m r -> p m r t"),
-                in_=w_raw[h][:].rearrange("p r (m t) -> p m r t", t=PACK),
-            )
+        w_dealt = w_raw[:].rearrange("p r (m t) -> p m r t", t=PACK)
+        for ts, ms, copy in (
+            (slice(0, 2), slice(0, W_SPLIT), nc.vector.tensor_copy),
+            (slice(0, 2), slice(W_SPLIT, P), nc.scalar.copy),
+            (slice(2, 4), slice(0, P), nc.scalar.copy),
+        ):
+            copy(out=w_bf[:, ts, ms, :].rearrange("p t m r -> p m r t"), in_=w_dealt[:, ms, :, ts])
         z = []
+        z_banks = []
         for t in range(PACK):
             w_codes = keep.tile([P, P], U32, name="w_codes%d" % t, align_bytes=64)
             w_plane = keep.tile([P, P], U8, name="w_plane%d" % t, align_bytes=64)
             nc.vector.quantize_mx(out=w_codes[:].bitcast(FP8X4), scales=w_plane[:], in_=w_bf[:, t, :, :].rearrange("p m r -> p (m r)"))
-            z_bank = psum.tile([P, T], F32, name="z_bank%d" % t)
+            z_bank = psum.tile([P, T], F32, name="z_bank%d" % t, tag="bank%d" % t)
             nc.tensor.matmul_mx(out=z_bank[:], lhsT=w_codes[:].bitcast(FP8X4), lhsT_scale=w_plane[:], rhs=xt_codes[:].bitcast(FP4X4), rhs_scale=xt_plane[:], start=True, stop=True)
             z_t = keep.tile([P, T], F32, name="z%d" % t)
-            nc.scalar.copy(out=z_t[:], in_=z_bank[:])
             z.append(z_t)
+            z_banks.append(z_bank)
+        for t, cols in ((0, slice(0, T)), (1, slice(0, T)), (2, slice(0, T - Z_REST)), (3, slice(0, T)), (2, slice(T - Z_REST, T))):
+            nc.scalar.copy(out=z[t][:, cols], in_=z_banks[t][:, cols])
 
-        q_banks = []
-        for c, (j0, width) in enumerate(CHUNKS):
-            per_bank = 512 // width
-            banks = []
-            for b in range(PACK // per_bank):
-                bank = psum.tile([P, per_bank, width], F32, name="q_bank%d_%d" % (c, b))
-                for i in range(per_bank):
-                    t = b * per_bank + i
+        nc.vector.tensor_copy(out=ws_dealt_plane[:].rearrange("p (t m) -> p t m", t=PACK), in_=ws_plane[:].rearrange("p (m t) -> p t m", t=PACK))
+
+        q_banks = {}
+        for pair in range(2):
+            for half in range(2):
+                bank = psum.tile([P, 2, HALF], F32, name="q_bank%d%d" % (pair, half))
+                for i in range(2):
+                    t = 2 * pair + i
                     nc.tensor.matmul_mx(
                         out=bank[:, i, :],
                         lhsT=ws_codes[:, 2 * P * t : 2 * P * (t + 1)].bitcast(FP4X4),
                         lhsT_scale=ws_dealt_plane[:, P * t : P * (t + 1)],
-                        rhs=sx_codes[:, j0 : j0 + width].bitcast(FP8X4),
-                        rhs_scale=sx_plane[:, j0 : j0 + width],
+                        rhs=sx_codes[:, half * HALF : (half + 1) * HALF].bitcast(FP8X4),
+                        rhs_scale=sx_plane[:, half * HALF : (half + 1) * HALF],
                         start=True,
                         stop=True,
                     )
-                banks.append(bank)
-            q_banks.append(banks)
+                q_banks[pair, half] = bank
 
         y_plane = keep.tile([P, J], U8, name="y_plane", align_bytes=64)
         out_rows = out_0.rearrange("(p t) j -> p t j", t=PACK)
         out_words = out_1[0].rearrange("p c r -> p (c r)").bitcast(I32)
-        tiles = []
-        for c, (j0, width) in enumerate(CHUNKS):
-            d = {}
-            for key in ("u", "d", "th", "y"):
-                d[key] = keep.tile([P, PACK, width], F32, name="%s%d" % (key, c))
-            d["pair"] = keep.tile([P, width, 2], F32, name="pair%d" % c)
-            d["sum"] = keep.tile([P, width], F32, name="sum%d" % c)
-            d["bf"] = keep.tile([P, width, PACK], BF16, name="bf%d" % c, align_bytes=64)
-            d["codes"] = keep.tile([P, width], U32, name="codes%d" % c, align_bytes=64)
-            tiles.append(d)
+        work = {}
+        for pair in range(2):
+            for half in range(2):
+                if (pair, half) == (1, 0):
+                    work[pair, half] = keep.tile([P, 2 * HALF], F32, name="work10", tag="stage_b", align_bytes=64)
+                else:
+                    work[pair, half] = keep.tile([P, 2 * HALF], F32, name="work%d%d" % (pair, half))
+        y = [keep.tile([P, PACK, HALF], F32, name="y%d" % half) for half in range(2)]
+        y_bf = [keep.tile([P, HALF, PACK], BF16, name="y_bf%d" % half, align_bytes=64) for half in range(2)]
+        y_codes = [keep.tile([P, HALF], U32, name="y_codes%d" % half, align_bytes=64) for half in range(2)]
 
-        def gather(c, t):
-            j0, width = CHUNKS[c]
-            nc.vector.tensor_copy(tiles[c]["u"][:, t, :], z[t][:].indirect(lists[:, j0 // 16 : (j0 + width) // 16]))
+        def members(pair, half):
+            return work[pair, half][:].rearrange("p (b g) -> p b g", g=GROUP)
 
-        def members(ap):
-            return ap.rearrange("p t (b g) -> p (t b) g", g=GROUP)
+        def gather(t, half):
+            nc.vector.tensor_copy(work[t // 2, half][:, (t % 2) * HALF : (t % 2 + 1) * HALF], z[t][:].indirect(lists[:, half * HALF // 16 : (half + 1) * HALF // 16]))
 
-        def pairs(c):
-            u = members(tiles[c]["u"][:])
-            nc.vector.tensor_tensor(tiles[c]["pair"][:], u[:, :, 0:2], u[:, :, 2:4], ADD)
+        means = {}
 
-        def sums(c):
-            pr = tiles[c]["pair"]
-            nc.vector.tensor_tensor(tiles[c]["sum"][:], pr[:, :, 0], pr[:, :, 1], ADD)
+        def minus_means(pair, halves, sums_bank, means_bank):
+            n = len(halves)
+            sums_t = psum.tile([P, n, P], F32, name="sums_t", tag="bank%d" % sums_bank)
+            for i, half in enumerate(halves):
+                for g in range(GROUP):
+                    nc.tensor.matmul(sums_t[:, i, :], lhsT=members(pair, half)[:, :, g], rhs=identity[:], is_transpose=True, start=g == 0, stop=g == GROUP - 1)
+            means_t = keep.tile([P, n, P], F32, name="means_t%d%d" % (pair, halves[0]))
+            nc.scalar.activation(out=means_t[:], in_=sums_t[:], func=COPY, scale=-1.0 / GROUP)
+            bank = psum.tile([P, n, P], F32, name="means", tag="bank%d" % means_bank)
+            for i, half in enumerate(halves):
+                nc.tensor.transpose(bank[:, i, :], means_t[:, i, :], identity[:])
+                means[pair, half] = bank[:, i, :]
 
-        def centre(c):
-            width = CHUNKS[c][1]
+        def centre_and_squash(pair, half, after):
+            u = members(pair, half)
+            centred = keep.tile([P, 2 * HALF], F32, name="centred", tag="z%d" % after)
+            nc.vector.tensor_tensor(centred[:].rearrange("p (b g) -> p b g", g=GROUP), means[pair, half].unsqueeze(2).to_broadcast(list(u.shape)), u, ADD)
+            nc.scalar.activation(out=work[pair, half][:], in_=centred[:], func=TANH)
+
+        def add_q(pair, half):
+            ts = slice(2 * pair, 2 * pair + 2)
             nc.vector.scalar_tensor_tensor(
-                out=members(tiles[c]["d"][:]),
-                in0=tiles[c]["sum"][:].unsqueeze(2).to_broadcast([P, width, GROUP]),
-                scalar=-1.0 / GROUP,
-                in1=members(tiles[c]["u"][:]),
+                out=y[half][:, ts, :].rearrange("p t j -> p (t j)"),
+                in0=q_banks[pair, half][:].rearrange("p t j -> p (t j)"),
+                scalar=0.5,
+                in1=work[pair, half][:],
                 op0=MULT,
                 op1=ADD,
             )
-            nc.scalar.activation(out=tiles[c]["th"][:], in_=tiles[c]["d"][:], func=TANH)
+            nc.sync.dma_start(out=out_rows[:, ts, half * HALF : (half + 1) * HALF], in_=y[half][:, ts, :])
 
-        def add_q(c, b):
-            per_bank = 512 // CHUNKS[c][1]
-            ts = slice(b * per_bank, (b + 1) * per_bank)
-            nc.vector.scalar_tensor_tensor(out=tiles[c]["y"][:, ts, :], in0=q_banks[c][b][:], scalar=0.5, in1=tiles[c]["th"][:, ts, :], op0=MULT, op1=ADD)
-
-        def store_y(c, engine_copy):
-            j0, width = CHUNKS[c]
-            nc.sync.dma_start(out=out_rows[:, :, j0 : j0 + width], in_=tiles[c]["y"][:])
+        def round_y(half, cols, engine_copy):
             engine_copy(
-                out=tiles[c]["bf"][:].rearrange("p (c i) t -> p c t i", i=4),
-                in_=tiles[c]["y"][:].rearrange("p t (c i) -> p c t i", i=4),
+                out=y_bf[half][:, cols, :].rearrange("p (c i) t -> p c t i", i=4),
+                in_=y[half][:, :, cols].rearrange("p t (c i) -> p c t i", i=4),
             )
 
-        def planes(c):
-            j0, width = CHUNKS[c]
-            nc.vector.quantize_mx(out=tiles[c]["codes"][:].bitcast(FP8X4), scales=y_plane[:, j0 : j0 + width], in_=tiles[c]["bf"][:].rearrange("p c t -> p (c t)"))
-            nc.sync.dma_start(out=out_words[:, j0 : j0 + width], in_=tiles[c]["codes"][:].bitcast(I32))
+        def planes(half):
+            cols = slice(half * HALF, (half + 1) * HALF)
+            nc.vector.quantize_mx(out=y_codes[half][:].bitcast(FP8X4), scales=y_plane[:, cols], in_=y_bf[half][:].rearrange("p c t -> p (c t)"))
+            nc.sync.dma_start(out=out_words[:, cols], in_=y_codes[half][:].bitcast(I32))
 
-        for t in range(PACK):
-            gather(0, t)
-        gather(1, 0)
-        pairs(0)
-        gather(1, 1)
-        sums(0)
-        gather(1, 2)
-        centre(0)
-        gather(1, 3)
-        gather(2, 0)
-        pairs(1)
-        gather(2, 1)
-        sums(1)
-        gather(2, 2)
-        centre(1)
-        gather(2, 3)
+        for t in range(2):
+            for half in range(2):
+                gather(t, half)
+        minus_means(0, (0, 1), 0, 1)
+        for half in range(2):
+            gather(3, half)
+            gather(2, half)
+            minus_means(1, (half,), (3, 0)[half], (2, 3)[half])
+        centre_and_squash(0, 0, 2)
+        centre_and_squash(0, 1, 3)
+        centre_and_squash(1, 0, 1)
         add_q(0, 0)
-        pairs(2)
-        add_q(0, 1)
-        store_y(0, nc.scalar.copy)
-        sums(2)
+        centre_and_squash(1, 1, 0)
         add_q(1, 0)
-        store_y(1, nc.scalar.copy)
-        centre(2)
+        round_y(0, slice(0, HALF), nc.scalar.copy)
+        add_q(0, 1)
+        add_q(1, 1)
+        round_y(1, slice(0, Y_SPLIT), nc.vector.tensor_copy)
+        round_y(1, slice(Y_SPLIT, HALF), nc.scalar.copy)
         planes(0)
-        add_q(2, 0)
         planes(1)
-        store_y(2, nc.vector.tensor_copy)
-        planes(2)
         for quad in range(4):
             queue = nc.scalar if quad % 2 else nc.sync
             queue.dma_start(out=out_2[0, 4 * quad : 4 * quad + 4, :].bitcast(I32), in_=y_plane[32 * quad : 32 * quad + 4, :].bitcast(I32))

@@ -23,7 +23,7 @@ GROUP = 4
 FLOPS = 2 * K * N * T + 2 * L * N * J
 HALF = J // 2
 W_SPLIT = 88
-Y_SPLIT = 176
+PIECES = ((0, 256), (256, 128), (384, 128))
 Z_REST = 64
 
 
@@ -39,7 +39,7 @@ def tile_list_head_members_and_group_pl_kernel(tc, xt_words, xt_scales, w, sx_wo
         psum = ctx.enter_context(tc.psum_pool(name="psum", bufs=1))
 
         lists = keep.tile([P, J // 16], U16, name="lists")
-        ws_plane = keep.tile([P, N], U8, name="ws_plane", tag="stage_b", align_bytes=64)
+        ws_plane = keep.tile([P, N], U8, name="ws_plane", tag="work01", align_bytes=64)
         xt_plane = keep.tile([P, T], U8, name="xt_plane", align_bytes=64)
         nc.gpsimd.memset(ws_plane[:].bitcast(I32), 0)
         identity = keep.tile([P, P], F32, name="identity")
@@ -50,19 +50,20 @@ def tile_list_head_members_and_group_pl_kernel(tc, xt_words, xt_scales, w, sx_wo
         w_rows = w.rearrange("(p r) n -> p r n", r=PACK)
         w_raw = keep.tile([P, PACK, N], F32, name="w_raw", tag="stage_w", align_bytes=64)
 
-        sx_codes = keep.tile([P, J], U32, name="sx_codes", align_bytes=64)
         nc.sync.dma_start(lists[:], offs)
         load_scales(nc.scalar, xt_plane, xt_scales)
         nc.sync.dma_start(out=ws_raw[:].bitcast(I32), in_=ws_words[0].bitcast(I32))
-        nc.sync.dma_start(out=xt_codes[:].bitcast(I32), in_=xt_words[0].bitcast(I32))
         nc.sync.dma_start(out=w_raw[:], in_=w_rows)
-        nc.sync.dma_start(out=sx_codes[:].bitcast(I32), in_=sx_words[0].rearrange("p c r -> p (c r)").bitcast(I32))
-        load_scales(nc.scalar, ws_plane, ws_scales)
+        nc.sync.dma_start(out=xt_codes[:].bitcast(I32), in_=xt_words[0].bitcast(I32))
+        load_scales(nc.sync, ws_plane, ws_scales)
 
         ws_codes = keep.tile([P, 2 * N], U8, name="ws_codes", align_bytes=64)
         ws_dealt_plane = keep.tile([P, N], U8, name="ws_dealt_plane", align_bytes=64)
         nc.vector.tensor_copy(out=ws_codes[:].rearrange("p (t m b) -> p t m b", t=PACK, b=2), in_=ws_raw[:].rearrange("p (m t b) -> p t m b", t=PACK, b=2))
-        sx_plane = keep.tile([P, J], U8, name="sx_plane", tag="stage_s", align_bytes=64)
+        sx = keep.tile([P, 5 * J], U8, name="sx", tag="stage_s", align_bytes=64)
+        sx_codes = sx[:, 0 : 4 * J].bitcast(U32)
+        sx_plane = sx[:, 4 * J : 5 * J]
+        nc.sync.dma_start(out=sx_codes.bitcast(I32), in_=sx_words[0].rearrange("p c r -> p (c r)").bitcast(I32))
         load_scales(nc.sync, sx_plane, sx_scales)
 
         w_bf = keep.tile([P, PACK, P, PACK], BF16, name="w_bf", align_bytes=64)
@@ -79,16 +80,112 @@ def tile_list_head_members_and_group_pl_kernel(tc, xt_words, xt_scales, w, sx_wo
             w_codes = keep.tile([P, P], U32, name="w_codes%d" % t, align_bytes=64)
             w_plane = keep.tile([P, P], U8, name="w_plane%d" % t, align_bytes=64)
             nc.vector.quantize_mx(out=w_codes[:].bitcast(FP8X4), scales=w_plane[:], in_=w_bf[:, t, :, :].rearrange("p m r -> p (m r)"))
-            z_bank = psum.tile([P, T], F32, name="z_bank%d" % t, tag="bank%d" % t)
-            nc.tensor.matmul_mx(out=z_bank[:], lhsT=w_codes[:].bitcast(FP8X4), lhsT_scale=w_plane[:], rhs=xt_codes[:].bitcast(FP4X4), rhs_scale=xt_plane[:], start=True, stop=True)
             z_t = keep.tile([P, T], F32, name="z%d" % t)
+            if t == 0:
+                for c0, tag, copy in ((0, "bank0", nc.scalar.copy), (T // 2, "bank3", nc.vector.tensor_copy)):
+                    z_bank = psum.tile([P, T // 2], F32, name="z_bank0", tag=tag)
+                    nc.tensor.matmul_mx(out=z_bank[:], lhsT=w_codes[:].bitcast(FP8X4), lhsT_scale=w_plane[:], rhs=xt_codes[:, 2 * c0 : 2 * c0 + T].bitcast(FP4X4), rhs_scale=xt_plane[:, c0 : c0 + T // 2], start=True, stop=True)
+                    copy(out=z_t[:, c0 : c0 + T // 2], in_=z_bank[:])
+            else:
+                z_bank = psum.tile([P, T], F32, name="z_bank%d" % t, tag="bank%d" % t)
+                nc.tensor.matmul_mx(out=z_bank[:], lhsT=w_codes[:].bitcast(FP8X4), lhsT_scale=w_plane[:], rhs=xt_codes[:].bitcast(FP4X4), rhs_scale=xt_plane[:], start=True, stop=True)
             z.append(z_t)
             z_banks.append(z_bank)
-        for t, cols in ((0, slice(0, T)), (1, slice(0, T)), (2, slice(0, T - Z_REST)), (3, slice(0, T)), (2, slice(T - Z_REST, T))):
+        for t, cols in ((1, slice(0, T)), (2, slice(0, T - Z_REST)), (3, slice(0, T)), (2, slice(T - Z_REST, T))):
             nc.scalar.copy(out=z[t][:, cols], in_=z_banks[t][:, cols])
 
         nc.vector.tensor_copy(out=ws_dealt_plane[:].rearrange("p (t m) -> p t m", t=PACK), in_=ws_plane[:].rearrange("p (m t) -> p t m", t=PACK))
 
+        y_plane = keep.tile([P, J], U8, name="y_plane", align_bytes=64)
+        out_rows = out_0.rearrange("(p t) j -> p t j", t=PACK)
+        out_words = out_1[0].rearrange("p c r -> p (c r)").bitcast(I32)
+        work = {}
+        for pair in range(2):
+            for half in range(2):
+                work[pair, half] = keep.tile([P, 2 * HALF], F32, name="work%d%d" % (pair, half), align_bytes=64)
+        y = [keep.tile([P, PACK, width], F32, name="y%d" % j0) for j0, width in PIECES]
+        y_bf = [keep.tile([P, width, PACK], BF16, name="y_bf%d" % j0, align_bytes=64) for j0, width in PIECES]
+        y_codes = [keep.tile([P, HALF], U32, name="y_codes%d" % half, align_bytes=64) for half in range(2)]
+
+        def members(pair, half):
+            return work[pair, half][:].rearrange("p (b g) -> p b g", g=GROUP)
+
+        def gather(t, half):
+            nc.vector.tensor_copy(work[t // 2, half][:, (t % 2) * HALF : (t % 2 + 1) * HALF], z[t][:].indirect(lists[:, half * HALF // 16 : (half + 1) * HALF // 16]))
+
+        means = {}
+
+        def group_sums(pair, halves, bank_tag):
+            sums_t = psum.tile([P, len(halves), P], F32, name="sums_t", tag=bank_tag)
+            for i, half in enumerate(halves):
+                for g in range(GROUP):
+                    nc.tensor.matmul(sums_t[:, i, :], lhsT=members(pair, half)[:, :, g], rhs=identity[:], is_transpose=True, start=g == 0, stop=g == GROUP - 1)
+            return sums_t
+
+        def minus_means(pair, halves, sums_t, bank_tag, means_tag):
+            means_t = keep.tile([P, len(halves), P], F32, name="means_t", tag=means_tag, align_bytes=64)
+            nc.scalar.activation(out=means_t[:], in_=sums_t[:], func=COPY, scale=-1.0 / GROUP)
+            bank = psum.tile([P, len(halves), P], F32, name="means", tag=bank_tag)
+            for i, half in enumerate(halves):
+                nc.tensor.transpose(bank[:, i, :], means_t[:, i, :], identity[:])
+                means[pair, half] = bank[:, i, :]
+
+        centred = {}
+        squashed = {}
+
+        def centre(pair, half, after):
+            u = members(pair, half)
+            centred[pair, half] = keep.tile([P, 2 * HALF], F32, name="centred", tag="z%d" % after)
+            nc.vector.tensor_tensor(centred[pair, half][:].rearrange("p (b g) -> p b g", g=GROUP), means[pair, half].unsqueeze(2).to_broadcast(list(u.shape)), u, ADD)
+
+        def squash(pair, half):
+            squashed[pair, half] = keep.tile([P, 2 * HALF], F32, name="squashed", tag="work%d%d" % (pair, half), align_bytes=64)
+            nc.scalar.activation(out=squashed[pair, half][:], in_=centred[pair, half][:], func=TANH)
+
+        def add_q(pair, piece):
+            j0, width = PIECES[piece]
+            half = j0 // HALF
+            cols = slice(j0 - half * HALF, j0 - half * HALF + width)
+            ts = slice(2 * pair, 2 * pair + 2)
+            nc.vector.scalar_tensor_tensor(
+                out=y[piece][:, ts, :],
+                in0=q_banks[pair, half][:, :, cols],
+                scalar=0.5,
+                in1=squashed[pair, half][:].rearrange("p (t j) -> p t j", t=2)[:, :, cols],
+                op0=MULT,
+                op1=ADD,
+            )
+
+        def store_y(piece, ts):
+            j0, width = PIECES[piece]
+            nc.sync.dma_start(out=out_rows[:, ts, j0 : j0 + width], in_=y[piece][:, ts, :])
+
+        def round_y(piece, engine_copy):
+            engine_copy(
+                out=y_bf[piece][:].rearrange("p (c i) t -> p c t i", i=4),
+                in_=y[piece][:].rearrange("p t (c i) -> p c t i", i=4),
+            )
+
+        def planes(piece):
+            j0, width = PIECES[piece]
+            cols = slice(j0, j0 + width)
+            half = j0 // HALF
+            codes = y_codes[half][:, j0 - half * HALF : j0 - half * HALF + width]
+            nc.vector.quantize_mx(out=codes.bitcast(FP8X4), scales=y_plane[:, cols], in_=y_bf[piece][:].rearrange("p c t -> p (c t)"))
+
+        def store_codes(half, queue):
+            queue.dma_start(out=out_words[:, half * HALF : (half + 1) * HALF], in_=y_codes[half][:].bitcast(I32))
+
+        for t in range(2):
+            for half in range(2):
+                gather(t, half)
+        minus_means(0, (0, 1), group_sums(0, (0, 1), "bank0"), "bank1", "means_t0")
+        gather(3, 0)
+        gather(2, 0)
+        minus_means(1, (0,), group_sums(1, (0,), "bank3"), "bank2", "means_t1")
+        gather(3, 1)
+        gather(2, 1)
+        last_sums = group_sums(1, (1,), "bank0")
         q_banks = {}
         for pair in range(2):
             for half in range(2):
@@ -106,91 +203,33 @@ def tile_list_head_members_and_group_pl_kernel(tc, xt_words, xt_scales, w, sx_wo
                     )
                 q_banks[pair, half] = bank
 
-        y_plane = keep.tile([P, J], U8, name="y_plane", align_bytes=64)
-        out_rows = out_0.rearrange("(p t) j -> p t j", t=PACK)
-        out_words = out_1[0].rearrange("p c r -> p (c r)").bitcast(I32)
-        work = {}
-        for pair in range(2):
-            for half in range(2):
-                if (pair, half) == (1, 0):
-                    work[pair, half] = keep.tile([P, 2 * HALF], F32, name="work10", tag="stage_b", align_bytes=64)
-                else:
-                    work[pair, half] = keep.tile([P, 2 * HALF], F32, name="work%d%d" % (pair, half))
-        y = [keep.tile([P, PACK, HALF], F32, name="y%d" % half) for half in range(2)]
-        y_bf = [keep.tile([P, HALF, PACK], BF16, name="y_bf%d" % half, align_bytes=64) for half in range(2)]
-        y_codes = [keep.tile([P, HALF], U32, name="y_codes%d" % half, align_bytes=64) for half in range(2)]
-
-        def members(pair, half):
-            return work[pair, half][:].rearrange("p (b g) -> p b g", g=GROUP)
-
-        def gather(t, half):
-            nc.vector.tensor_copy(work[t // 2, half][:, (t % 2) * HALF : (t % 2 + 1) * HALF], z[t][:].indirect(lists[:, half * HALF // 16 : (half + 1) * HALF // 16]))
-
-        means = {}
-
-        def minus_means(pair, halves, sums_bank, means_bank):
-            n = len(halves)
-            sums_t = psum.tile([P, n, P], F32, name="sums_t", tag="bank%d" % sums_bank)
-            for i, half in enumerate(halves):
-                for g in range(GROUP):
-                    nc.tensor.matmul(sums_t[:, i, :], lhsT=members(pair, half)[:, :, g], rhs=identity[:], is_transpose=True, start=g == 0, stop=g == GROUP - 1)
-            means_t = keep.tile([P, n, P], F32, name="means_t%d%d" % (pair, halves[0]))
-            nc.scalar.activation(out=means_t[:], in_=sums_t[:], func=COPY, scale=-1.0 / GROUP)
-            bank = psum.tile([P, n, P], F32, name="means", tag="bank%d" % means_bank)
-            for i, half in enumerate(halves):
-                nc.tensor.transpose(bank[:, i, :], means_t[:, i, :], identity[:])
-                means[pair, half] = bank[:, i, :]
-
-        def centre_and_squash(pair, half, after):
-            u = members(pair, half)
-            centred = keep.tile([P, 2 * HALF], F32, name="centred", tag="z%d" % after)
-            nc.vector.tensor_tensor(centred[:].rearrange("p (b g) -> p b g", g=GROUP), means[pair, half].unsqueeze(2).to_broadcast(list(u.shape)), u, ADD)
-            nc.scalar.activation(out=work[pair, half][:], in_=centred[:], func=TANH)
-
-        def add_q(pair, half):
-            ts = slice(2 * pair, 2 * pair + 2)
-            nc.vector.scalar_tensor_tensor(
-                out=y[half][:, ts, :].rearrange("p t j -> p (t j)"),
-                in0=q_banks[pair, half][:].rearrange("p t j -> p (t j)"),
-                scalar=0.5,
-                in1=work[pair, half][:],
-                op0=MULT,
-                op1=ADD,
-            )
-            nc.sync.dma_start(out=out_rows[:, ts, half * HALF : (half + 1) * HALF], in_=y[half][:, ts, :])
-
-        def round_y(half, cols, engine_copy):
-            engine_copy(
-                out=y_bf[half][:, cols, :].rearrange("p (c i) t -> p c t i", i=4),
-                in_=y[half][:, :, cols].rearrange("p t (c i) -> p c t i", i=4),
-            )
-
-        def planes(half):
-            cols = slice(half * HALF, (half + 1) * HALF)
-            nc.vector.quantize_mx(out=y_codes[half][:].bitcast(FP8X4), scales=y_plane[:, cols], in_=y_bf[half][:].rearrange("p c t -> p (c t)"))
-            nc.sync.dma_start(out=out_words[:, cols], in_=y_codes[half][:].bitcast(I32))
-
-        for t in range(2):
-            for half in range(2):
-                gather(t, half)
-        minus_means(0, (0, 1), 0, 1)
-        for half in range(2):
-            gather(3, half)
-            gather(2, half)
-            minus_means(1, (half,), (3, 0)[half], (2, 3)[half])
-        centre_and_squash(0, 0, 2)
-        centre_and_squash(0, 1, 3)
-        centre_and_squash(1, 0, 1)
+        centre(0, 0, 2)
+        squash(0, 0)
+        centre(0, 1, 3)
+        minus_means(1, (1,), last_sums, "bank3", "work01")
+        centre(1, 0, 1)
+        squash(1, 0)
+        squash(0, 1)
         add_q(0, 0)
-        centre_and_squash(1, 1, 0)
+        store_y(0, slice(0, 2))
+        centre(1, 1, 0)
+        squash(1, 1)
         add_q(1, 0)
-        round_y(0, slice(0, HALF), nc.scalar.copy)
+        store_y(0, slice(2, 4))
+        round_y(0, nc.scalar.copy)
         add_q(0, 1)
+        add_q(0, 2)
         add_q(1, 1)
-        round_y(1, slice(0, Y_SPLIT), nc.vector.tensor_copy)
-        round_y(1, slice(Y_SPLIT, HALF), nc.scalar.copy)
+        store_y(1, slice(0, 4))
+        round_y(1, nc.scalar.copy)
+        add_q(1, 2)
+        store_y(2, slice(0, 4))
         planes(0)
+        store_codes(0, nc.sync)
+        round_y(2, nc.vector.tensor_copy)
         planes(1)
+        planes(2)
+        store_codes(1, nc.scalar)
         for quad in range(4):
-            queue = nc.scalar if quad % 2 else nc.sync
+            queue = nc.scalar if quad == 3 else nc.sync
             queue.dma_start(out=out_2[0, 4 * quad : 4 * quad + 4, :].bitcast(I32), in_=y_plane[32 * quad : 32 * quad + 4, :].bitcast(I32))

from contextlib import ExitStack

import concourse.mybir as mybir
from concourse.masks import make_identity

F32 = mybir.dt.float32
BF16 = mybir.dt.bfloat16
I32 = mybir.dt.int32
U32 = mybir.dt.uint32
U16 = mybir.dt.uint16
U8 = mybir.dt.uint8
FP8X4 = mybir.dt.float8_e4m3fn_x4
FP4X4 = mybir.dt.float4_e2m1fn_x4
ADD = mybir.AluOpType.add
MULT = mybir.AluOpType.mult
TANH = mybir.ActivationFunctionType.Tanh
COPY = mybir.ActivationFunctionType.Copy

P = 128
PACK = 4
K = T = J = L = N = 512
GROUP = 4
FLOPS = 2 * K * N * T + 2 * L * N * J
HALF = J // 2
W_SPLIT = 88
PIECES = ((0, 256), (256, 128), (384, 128))
Z_REST = 64


def load_scales(queue, plane, rows):
    for quad in range(4):
        queue.dma_start(out=plane[32 * quad : 32 * quad + 4, :].bitcast(I32), in_=rows[0, 4 * quad : 4 * quad + 4, :].bitcast(I32))


def tile_list_head_members_and_group_pl_kernel(tc, xt_words, xt_scales, w, sx_words, sx_scales, ws_words, ws_scales, offs, out_0, out_1, out_2):
    nc = tc.nc
    with ExitStack() as ctx:
        keep = ctx.enter_context(tc.tile_pool(name="keep", bufs=1))
        psum = ctx.enter_context(tc.psum_pool(name="psum", bufs=1))

        lists = keep.tile([P, J // 16], U16, name="lists")
        ws_plane = keep.tile([P, N], U8, name="ws_plane", tag="work01", align_bytes=64)
        xt_plane = keep.tile([P, T], U8, name="xt_plane", align_bytes=64)
        nc.gpsimd.memset(ws_plane[:].bitcast(I32), 0)
        identity = keep.tile([P, P], F32, name="identity")
        make_identity(nc, identity[:])

        ws_raw = keep.tile([P, 2 * N], U8, name="ws_raw", tag="stage_s", align_bytes=64)
        xt_codes = keep.tile([P, 2 * T], U8, name="xt_codes", align_bytes=64)
        w_rows = w.rearrange("(p r) n -> p r n", r=PACK)
        w_raw = keep.tile([P, PACK, N], F32, name="w_raw", tag="stage_w", align_bytes=64)

        nc.sync.dma_start(lists[:], offs)
        load_scales(nc.scalar, xt_plane, xt_scales)
        nc.sync.dma_start(out=ws_raw[:].bitcast(I32), in_=ws_words[0].bitcast(I32))
        nc.sync.dma_start(out=w_raw[:], in_=w_rows)
        nc.sync.dma_start(out=xt_codes[:].bitcast(I32), in_=xt_words[0].bitcast(I32))
        load_scales(nc.sync, ws_plane, ws_scales)

        ws_codes = keep.tile([P, 2 * N], U8, name="ws_codes", align_bytes=64)
        ws_dealt_plane = keep.tile([P, N], U8, name="ws_dealt_plane", align_bytes=64)
        nc.vector.tensor_copy(out=ws_codes[:].rearrange("p (t m b) -> p t m b", t=PACK, b=2), in_=ws_raw[:].rearrange("p (m t b) -> p t m b", t=PACK, b=2))
        sx = keep.tile([P, 5 * J], U8, name="sx", tag="stage_s", align_bytes=64)
        sx_codes = sx[:, 0 : 4 * J].bitcast(U32)
        sx_plane = sx[:, 4 * J : 5 * J]
        nc.sync.dma_start(out=sx_codes.bitcast(I32), in_=sx_words[0].rearrange("p c r -> p (c r)").bitcast(I32))
        load_scales(nc.sync, sx_plane, sx_scales)

        w_bf = keep.tile([P, PACK, P, PACK], BF16, name="w_bf", align_bytes=64)
        w_dealt = w_raw[:].rearrange("p r (m t) -> p m r t", t=PACK)
        for ts, ms, copy in (
            (slice(0, 2), slice(0, W_SPLIT), nc.vector.tensor_copy),
            (slice(0, 2), slice(W_SPLIT, P), nc.scalar.copy),
            (slice(2, 4), slice(0, P), nc.scalar.copy),
        ):
            copy(out=w_bf[:, ts, ms, :].rearrange("p t m r -> p m r t"), in_=w_dealt[:, ms, :, ts])
        z = []
        z_banks = []
        for t in range(PACK):
            w_codes = keep.tile([P, P], U32, name="w_codes%d" % t, align_bytes=64)
            w_plane = keep.tile([P, P], U8, name="w_plane%d" % t, align_bytes=64)
            nc.vector.quantize_mx(out=w_codes[:].bitcast(FP8X4), scales=w_plane[:], in_=w_bf[:, t, :, :].rearrange("p m r -> p (m r)"))
            z_t = keep.tile([P, T], F32, name="z%d" % t)
            if t == 0:
                for c0, tag, copy in ((0, "bank0", nc.scalar.copy), (T // 2, "bank3", nc.vector.tensor_copy)):
                    z_bank = psum.tile([P, T // 2], F32, name="z_bank0", tag=tag)
                    nc.tensor.matmul_mx(out=z_bank[:], lhsT=w_codes[:].bitcast(FP8X4), lhsT_scale=w_plane[:], rhs=xt_codes[:, 2 * c0 : 2 * c0 + T].bitcast(FP4X4), rhs_scale=xt_plane[:, c0 : c0 + T // 2], start=True, stop=True)
                    copy(out=z_t[:, c0 : c0 + T // 2], in_=z_bank[:])
            else:
                z_bank = psum.tile([P, T], F32, name="z_bank%d" % t, tag="bank%d" % t)
                nc.tensor.matmul_mx(out=z_bank[:], lhsT=w_codes[:].bitcast(FP8X4), lhsT_scale=w_plane[:], rhs=xt_codes[:].bitcast(FP4X4), rhs_scale=xt_plane[:], start=True, stop=True)
            z.append(z_t)
            z_banks.append(z_bank)
        for t, cols in ((1, slice(0, T)), (2, slice(0, T - Z_REST)), (3, slice(0, T)), (2, slice(T - Z_REST, T))):
            nc.scalar.copy(out=z[t][:, cols], in_=z_banks[t][:, cols])

        nc.vector.tensor_copy(out=ws_dealt_plane[:].rearrange("p (t m) -> p t m", t=PACK), in_=ws_plane[:].rearrange("p (m t) -> p t m", t=PACK))

        y_plane = keep.tile([P, J], U8, name="y_plane", align_bytes=64)
        out_rows = out_0.rearrange("(p t) j -> p t j", t=PACK)
        out_words = out_1[0].rearrange("p c r -> p (c r)").bitcast(I32)
        work = {}
        for pair in range(2):
            for half in range(2):
                work[pair, half] = keep.tile([P, 2 * HALF], F32, name="work%d%d" % (pair, half), align_bytes=64)
        y = [keep.tile([P, PACK, width], F32, name="y%d" % j0) for j0, width in PIECES]
        y_bf = [keep.tile([P, width, PACK], BF16, name="y_bf%d" % j0, align_bytes=64) for j0, width in PIECES]
        y_codes = [keep.tile([P, HALF], U32, name="y_codes%d" % half, align_bytes=64) for half in range(2)]

        def members(pair, half):
            return work[pair, half][:].rearrange("p (b g) -> p b g", g=GROUP)

        def gather(t, half):
            nc.vector.tensor_copy(work[t // 2, half][:, (t % 2) * HALF : (t % 2 + 1) * HALF], z[t][:].indirect(lists[:, half * HALF // 16 : (half + 1) * HALF // 16]))

        means = {}

        def group_sums(pair, halves, bank_tag):
            sums_t = psum.tile([P, len(halves), P], F32, name="sums_t", tag=bank_tag)
            for i, half in enumerate(halves):
                for g in range(GROUP):
                    nc.tensor.matmul(sums_t[:, i, :], lhsT=members(pair, half)[:, :, g], rhs=identity[:], is_transpose=True, start=g == 0, stop=g == GROUP - 1)
            return sums_t

        def minus_means(pair, halves, sums_t, bank_tag, means_tag):
            means_t = keep.tile([P, len(halves), P], F32, name="means_t", tag=means_tag, align_bytes=64)
            nc.scalar.activation(out=means_t[:], in_=sums_t[:], func=COPY, scale=-1.0 / GROUP)
            bank = psum.tile([P, len(halves), P], F32, name="means", tag=bank_tag)
            for i, half in enumerate(halves):
                nc.tensor.transpose(bank[:, i, :], means_t[:, i, :], identity[:])
                means[pair, half] = bank[:, i, :]

        centred = {}
        squashed = {}

        def centre(pair, half, after):
            u = members(pair, half)
            centred[pair, half] = keep.tile([P, 2 * HALF], F32, name="centred", tag="z%d" % after)
            nc.vector.tensor_tensor(centred[pair, half][:].rearrange("p (b g) -> p b g", g=GROUP), means[pair, half].unsqueeze(2).to_broadcast(list(u.shape)), u, ADD)

        def squash(pair, half):
            squashed[pair, half] = keep.tile([P, 2 * HALF], F32, name="squashed", tag="work%d%d" % (pair, half), align_bytes=64)
            nc.scalar.activation(out=squashed[pair, half][:], in_=centred[pair, half][:], func=TANH)

        def add_q(pair, piece):
            j0, width = PIECES[piece]
            half = j0 // HALF
            cols = slice(j0 - half * HALF, j0 - half * HALF + width)
            ts = slice(2 * pair, 2 * pair + 2)
            nc.vector.scalar_tensor_tensor(
                out=y[piece][:, ts, :],
                in0=q_banks[pair, half][:, :, cols],
                scalar=0.5,
                in1=squashed[pair, half][:].rearrange("p (t j) -> p t j", t=2)[:, :, cols],
                op0=MULT,
                op1=ADD,
            )

        def store_y(piece, ts):
            j0, width = PIECES[piece]
            nc.sync.dma_start(out=out_rows[:, ts, j0 : j0 + width], in_=y[piece][:, ts, :])

        def round_y(piece, engine_copy):
            engine_copy(
                out=y_bf[piece][:].rearrange("p (c i) t -> p c t i", i=4),
                in_=y[piece][:].rearrange("p t (c i) -> p c t i", i=4),
            )

        def planes(piece):
            j0, width = PIECES[piece]
            cols = slice(j0, j0 + width)
            half = j0 // HALF
            codes = y_codes[half][:, j0 - half * HALF : j0 - half * HALF + width]
            nc.vector.quantize_mx(out=codes.bitcast(FP8X4), scales=y_plane[:, cols], in_=y_bf[piece][:].rearrange("p c t -> p (c t)"))

        def store_codes(half, queue):
            queue.dma_start(out=out_words[:, half * HALF : (half + 1) * HALF], in_=y_codes[half][:].bitcast(I32))

        for t in range(2):
            for half in range(2):
                gather(t, half)
        minus_means(0, (0, 1), group_sums(0, (0, 1), "bank0"), "bank1", "means_t0")
        gather(3, 0)
        gather(2, 0)
        minus_means(1, (0,), group_sums(1, (0,), "bank3"), "bank2", "means_t1")
        gather(3, 1)
        gather(2, 1)
        last_sums = group_sums(1, (1,), "bank0")
        q_banks = {}
        for pair in range(2):
            for half in range(2):
                bank = psum.tile([P, 2, HALF], F32, name="q_bank%d%d" % (pair, half))
                for i in range(2):
                    t = 2 * pair + i
                    nc.tensor.matmul_mx(
                        out=bank[:, i, :],
                        lhsT=ws_codes[:, 2 * P * t : 2 * P * (t + 1)].bitcast(FP4X4),
                        lhsT_scale=ws_dealt_plane[:, P * t : P * (t + 1)],
                        rhs=sx_codes[:, half * HALF : (half + 1) * HALF].bitcast(FP8X4),
                        rhs_scale=sx_plane[:, half * HALF : (half + 1) * HALF],
                        start=True,
                        stop=True,
                    )
                q_banks[pair, half] = bank

        centre(0, 0, 2)
        squash(0, 0)
        centre(0, 1, 3)
        minus_means(1, (1,), last_sums, "bank3", "work01")
        centre(1, 0, 1)
        squash(1, 0)
        squash(0, 1)
        add_q(0, 0)
        store_y(0, slice(0, 2))
        centre(1, 1, 0)
        squash(1, 1)
        add_q(1, 0)
        store_y(0, slice(2, 4))
        round_y(0, nc.scalar.copy)
        add_q(0, 1)
        add_q(0, 2)
        add_q(1, 1)
        store_y(1, slice(0, 4))
        round_y(1, nc.scalar.copy)
        add_q(1, 2)
        store_y(2, slice(0, 4))
        planes(0)
        store_codes(0, nc.sync)
        round_y(2, nc.vector.tensor_copy)
        planes(1)
        planes(2)
        store_codes(1, nc.scalar)
        for quad in range(4):
            queue = nc.scalar if quad == 3 else nc.sync
            queue.dma_start(out=out_2[0, 4 * quad : 4 * quad + 4, :].bitcast(I32), in_=y_plane[32 * quad : 32 * quad + 4, :].bitcast(I32))
